import numpy as np
import ml_dtypes


def mxq(x, axis, fmt="e4m3"):
    dtype, down = {"e4m3": (ml_dtypes.float8_e4m3fn, 7), "e5m2": (ml_dtypes.float8_e5m2, 14)}[fmt]
    v = np.moveaxis(np.asarray(x, np.float32).astype(ml_dtypes.bfloat16).astype(np.float64), axis, -1)
    blocks = v.reshape(v.shape[:-1] + (-1, 32))
    amax = np.abs(blocks).max(-1, keepdims=True)
    byte = np.maximum(np.where(amax > 0, np.frexp(amax)[1] - 1 + 127, 0) - down, 1)
    scale = np.exp2(byte - 127.0)
    codes = (blocks / scale).astype(np.float32).astype(dtype).astype(np.float64)
    return np.moveaxis((codes * scale).reshape(v.shape), -1, axis)


WIDE = False


def mx_kscale(k):
    if not WIDE:
        return np.ones(k)
    levels = np.array([10, -10, 5, -5, 0])
    if k % 512:
        return np.exp2(np.random.permutation(np.resize(levels, k // 32))).repeat(32)
    a = np.empty((k // 512, 16))
    for p in range(k // 512):
        a[p, :8] = np.random.permutation(np.resize(levels, 8))
        for g in range(8):
            far = levels[np.abs(levels - a[p, g]) >= 10]
            a[p, g + 8] = far[np.random.randint(len(far))]
    return np.exp2(a.ravel()).repeat(32)


def f64(x):
    return np.asarray(x).astype(np.float64)


def striped(idx):
    return np.tile(idx.reshape(-1, 16).T, (8, 1)).astype(np.uint16)


def unstriped(offs):
    return offs[:16].T.reshape(-1).astype(np.int64)


def striped8(idx):
    return np.concatenate([x.reshape(-1, 16).T for x in idx]).astype(np.uint16)


def runs(offs, k):
    lists = np.stack([offs[16 * r : 16 * r + 16].T.reshape(-1) for r in range(8)]).astype(np.int64)
    return lists[np.arange(k) % 512 // 64]


def pack_weight(w):
    k, n = w.shape
    w = f64(np.asarray(w, np.float32).astype(ml_dtypes.bfloat16)).reshape(k // 32, 32, n)
    amax = np.abs(w).max(1)
    byte = np.clip(np.where(amax > 0, np.frexp(amax)[1] - 1 + 127 - 7, 1), 1, 254)
    scaled = (w * np.exp2(127.0 - byte)[:, None, :]).reshape(k, n).astype(np.float32)
    words = np.ascontiguousarray(scaled.reshape(k // 512, 128, 4, n).transpose(0, 1, 3, 2)).astype(ml_dtypes.float8_e4m3fn).view(np.uint8)
    return words, np.ascontiguousarray(byte.astype(np.uint8).reshape(k // 512, 16, n))


def unpack_weight(words, scales):
    g, p, n, _ = words.shape
    vals = np.ascontiguousarray(words).view(ml_dtypes.float8_e4m3fn).astype(np.float64) * np.repeat(np.exp2(scales.astype(np.float64) - 127.0), 8, axis=1)[..., None]
    return vals.transpose(0, 1, 3, 2).reshape(g * 512, n)


K, T, S, N, H, W = 512, 2048, 512, 512, 512, 256


def setup_inputs():
    n = np.random.standard_normal
    s = mx_kscale(K)[:, None]
    u = mx_kscale(H)
    packed_xT = pack_weight(n((K, T)) * s)
    return {
        "x_words": packed_xT[0],
        "x_scales": packed_xT[1],
        "w1": (n((K, H)) / np.sqrt(K) / s).astype(np.float32),
        "w2": (n((K, H)) / np.sqrt(K) / s).astype(np.float32),
        "w3": (n((K, H)) / np.sqrt(K) / s).astype(np.float32),
        "gn": (np.random.uniform(0.5, 1.5, (H, 1)) * u[:, None]).astype(np.float32),
        "w4": (n((H, N)) / np.sqrt(H) / u[:, None]).astype(np.float32),
        "offs": striped(np.random.permutation(T)[:S]),
        "two": striped(np.random.permutation(T)[:S]),
        "three": striped(np.random.permutation(T)[:S]),
        "n1": striped8(np.stack([np.random.permutation(S)[:W] for _ in range(8)])),
        "n2": striped8(np.stack([np.random.permutation(S)[:W] for _ in range(8)])),
        "n3": striped8(np.stack([np.random.permutation(S) for _ in range(8)])),
        "n4": striped8(np.stack([np.random.permutation(S) for _ in range(8)])),
        "n5": striped8(np.stack([np.random.permutation(S) for _ in range(8)])),
        "n6": striped8(np.stack([np.random.permutation(S) for _ in range(8)])),
        "n7": striped8(np.stack([np.random.permutation(S) for _ in range(8)])),
    }


def reference(x_words, x_scales, w1, w2, w3, gn, w4, offs, two, three, n1, n2, n3, n4, n5, n6, n7):
    x_two = unpack_weight(x_words, x_scales)[:, unstriped(two)]
    d = mxq(f64(w2), 0, "e4m3").T @ x_two
    xq = unpack_weight(x_words, x_scales)[:, unstriped(offs)]
    y = mxq(f64(w1), 0, "e4m3").T @ xq
    ra = d[np.arange(H)[:, None], runs(n2, H)] - (0.5 * (y[np.arange(H)[:, None], runs(n1, H)]))
    m1 = y.copy()
    m1[np.arange(H)[:, None], runs(n1, H)] = ra
    x_three = unpack_weight(x_words, x_scales)[:, unstriped(three)]
    b = mxq(f64(w3), 0, "e4m3").T @ x_three
    z = f64(gn) * ((m1 - (m1[np.arange(H)[:, None], runs(n3, H)])) / (np.abs(b) + np.abs(b[np.arange(H)[:, None], runs(n4, H)]) + 0.5))
    h = mxq(f64(w4), 0, "e4m3").T @ mxq(z, 0, "e4m3")
    return h + h[np.arange(N)[:, None], runs(n5, N)] - (np.maximum(h[np.arange(N)[:, None], runs(n6, N)], h[np.arange(N)[:, None], runs(n7, N)]))

@@ -1,0 +1,317 @@
+from contextlib import ExitStack
+
+import concourse.mybir as mybir
+from concourse.masks import make_identity
+
+F32 = mybir.dt.float32
+BF16 = mybir.dt.bfloat16
+I32 = mybir.dt.int32
+U32 = mybir.dt.uint32
+U16 = mybir.dt.uint16
+U8 = mybir.dt.uint8
+FP8X4 = mybir.dt.float8_e4m3fn_x4
+ALU = mybir.AluOpType
+ACT = mybir.ActivationFunctionType
+
+P = 128
+PACK = 4
+K, T, S, H, N, W = 512, 2048, 512, 512, 512, 256
+HALF = S // 2
+FLOPS = 2 * (3 * K * H * S + H * N * S)
+
+
+def tile_picked_trioputbnormbtrim_none_p_kernel(
+    tc, x_words, x_scales, w1, w2, w3, gn, w4, offs, two, three, n1, n2, n3, n4, n5, n6, n7, out
+):
+    nc = tc.nc
+    with ExitStack() as ctx:
+        keep = ctx.enter_context(tc.tile_pool(name="keep", bufs=1))
+        work = ctx.enter_context(tc.tile_pool(name="work", bufs=2))
+        psum = ctx.enter_context(tc.psum_pool(name="psum", bufs=1))
+
+        def load_list(src, name):
+            tile = keep.tile(list(src.shape), U16, name=name)
+            nc.sync.dma_start(tile[:], src)
+            return tile
+
+        def load_weight_half(w, half, name):
+            raw = keep.tile([P, PACK, HALF], F32, name=name)
+            nc.sync.dma_start(raw[:], w.rearrange("(p j) c -> p j c", j=PACK)[:, :, half * HALF : (half + 1) * HALF])
+            return raw
+
+        def load_weight(w, name):
+            raw = keep.tile([P, PACK, H], F32, name=name)
+            nc.sync.dma_start(raw[:], w.rearrange("(p j) c -> p j c", j=PACK))
+            return raw
+
+        def half_of(lst, half):
+            return lst[:, half * (HALF // 16) : (half + 1) * (HALF // 16)]
+
+        def cols(half):
+            return slice(half * HALF, (half + 1) * HALF)
+
+        x_plane = keep.tile([P, T], U8, name="x_plane", align_bytes=64)
+        nc.vector.memset(x_plane[:].bitcast(I32), 0)
+        three_t = load_list(three, "three_t")
+        x_codes = keep.tile([P, T], U32, name="x_codes", align_bytes=64)
+        nc.sync.dma_start(x_codes[:].bitcast(I32), x_words[0].rearrange("p n t -> p (n t)").bitcast(I32))
+        for q in range(4):
+            nc.scalar.dma_start(x_plane[32 * q : 32 * q + 4, :].bitcast(I32), x_scales[0, 4 * q : 4 * q + 4, :].bitcast(I32))
+        w3_raw = [load_weight_half(w3, h, "w3_raw%d" % h) for h in range(2)]
+        w1_raw = [load_weight_half(w1, 0, "w1_raw0")]
+        offs_t = load_list(offs, "offs_t")
+        w1_raw.append(load_weight_half(w1, 1, "w1_raw1"))
+        n4_t = load_list(n4, "n4_t")
+        two_t = load_list(two, "two_t")
+        w2_raw = load_weight(w2, "w2_raw")
+        gain_rows = keep.tile([P, P], F32, name="gain_rows")
+        nc.gpsimd.memset(gain_rows[:], 0.0)
+        nc.sync.dma_start(
+            gain_rows[0:4, :].rearrange("u (g r) -> u g r", g=8), gn.rearrange("(g u r) o -> u g (r o)", g=8, u=4)
+        )
+        n1_t = load_list(n1, "n1_t")
+        n2_t = load_list(n2, "n2_t")
+        w4_raw = load_weight(w4, "w4_raw")
+        n3_t = load_list(n3, "n3_t")
+        n5_t = load_list(n5, "n5_t")
+        n6_t = load_list(n6, "n6_t")
+        n7_t = load_list(n7, "n7_t")
+        ident = keep.tile([P, P], F32, name="ident")
+        make_identity(nc, ident[:])
+
+        def pick_words(lst, name):
+            words = keep.tile([P, S], U32, name=name, align_bytes=64)
+            nc.vector.tensor_copy(words[:], x_codes[:].indirect(lst[:]))
+            return words
+
+        def pick_scales(lst, name):
+            plane = keep.tile([P, S], U8, name=name, align_bytes=64)
+            nc.vector.tensor_copy(plane[:], x_plane[:].indirect(lst[:]))
+            return plane
+
+        def grouped_tile(name):
+            return keep.tile([P, H * PACK], BF16, name=name, align_bytes=64)
+
+        def round_by_runs(copy, grouped, raw, g0, groups):
+            dst = grouped[:].rearrange("p (u g r j) -> p g u r j", u=4, g=8, j=PACK)[:, g0 : g0 + groups]
+            copy(dst, raw.rearrange("p j (g u r) -> p g u r j", g=groups, u=4))
+
+        def quantise(grouped, width, name):
+            codes = keep.tile([P, width], U32, name=name + "_codes", align_bytes=64)
+            plane = keep.tile([P, width], U8, name=name + "_plane", align_bytes=64)
+            nc.vector.quantize_mx(out=codes[:].bitcast(FP8X4), scales=plane[:], in_=grouped)
+            return codes, plane
+
+        def product(acc, weights, u, moving):
+            m = slice(u * P, (u + 1) * P)
+            nc.tensor.matmul_mx(
+                out=acc,
+                lhsT=weights[0][:, m].bitcast(FP8X4),
+                lhsT_scale=weights[1][:, m],
+                rhs=moving[0][:].bitcast(FP8X4),
+                rhs_scale=moving[1][:],
+                start=True,
+                stop=True,
+            )
+
+        def bank_of(name, group, k):
+            return psum.tile([P, S], F32, name=name, tag="%s%d" % (group, k))
+
+        def turn_into(bank, src, first, last):
+            for jb in range(4):
+                blk = slice(jb * P, (jb + 1) * P)
+                nc.tensor.matmul(
+                    bank[:, blk], lhsT=src[:, blk], rhs=ident[:], is_transpose=True,
+                    start=(first and jb == 0), stop=(last and jb == 3),
+                )
+
+        def fetch_scalar(dst, window, lst, factor):
+            nc.scalar.activation(dst, window[:].indirect(lst), ACT.Copy, scale=factor)
+
+        def fetch_vector(dst, window, lst, factor):
+            nc.vector.tensor_scalar(dst, window[:].indirect(lst), factor, 0.0, ALU.mult, ALU.add)
+
+        x3 = [pick_words(three_t, "x3_words"), pick_scales(three_t, "x3_plane")]
+        w3_g = grouped_tile("w3_g")
+        round_by_runs(nc.scalar.copy, w3_g, w3_raw[0][:], 0, 4)
+        round_by_runs(nc.vector.tensor_copy, w3_g, w3_raw[1][:], 4, 4)
+        w3_q = quantise(w3_g[:], H, "w3")
+        w1_g = grouped_tile("w1_g")
+        round_by_runs(nc.scalar.copy, w1_g, w1_raw[0][:], 0, 4)
+        xo = [pick_words(offs_t, "xo_words"), pick_scales(offs_t, "xo_plane")]
+        round_by_runs(nc.vector.tensor_copy, w1_g, w1_raw[1][:], 4, 4)
+        w1_q = quantise(w1_g[:], H, "w1")
+
+        m1 = [keep.tile([P, 2 * S], F32, name="m1_%d" % u, align_bytes=64) for u in range(4)]
+        h = [keep.tile([P, 2 * S], F32, name="h%d" % t) for t in range(4)]
+        rec = [keep.tile([P, S], F32, name="rec%d" % u) for u in range(4)]
+        dens = []
+
+        def sizes(u):
+            bank = bank_of("bb", "left", u % 2)
+            product(bank[:], w3_q, u, x3)
+            size = work.tile([P, S], F32, name="size")
+            nc.scalar.activation(size[:], bank[:], ACT.Abs)
+            size_far = m1[u][:, S:]
+            for half in range(2):
+                fetch_scalar(size_far[:, cols(half)], size, half_of(n4_t, half), 1.0)
+            den = bank_of("den", "right", u % 2)
+            turn_into(den, size, True, False)
+            turn_into(den, size_far, False, True)
+            dens.append(den)
+
+        def invert(u):
+            root = keep.tile([P, S], F32, name="root%d" % u)
+            nc.scalar.activation(root[:], dens[u][:], ACT.Abs_reciprocal_sqrt, bias=0.5)
+            nc.scalar.activation(rec[u][:], root[:], ACT.Square)
+
+        for u in range(4):
+            sizes(u)
+            if u > 0:
+                invert(u - 1)
+        invert(3)
+
+        xt = [pick_words(two_t, "xt_words"), pick_scales(two_t, "xt_plane")]
+        w2_g = grouped_tile("w2_g")
+        round_by_runs(nc.vector.tensor_copy, w2_g, w2_raw[:], 0, 8)
+        w2_q = quantise(w2_g[:], H, "w2")
+
+        gain_bank = bank_of("gb", "row", 3)
+        nc.tensor.transpose(gain_bank[:, 0:P], gain_rows[:], ident[:])
+        gain = keep.tile([P, 4], F32, name="gain")
+        nc.vector.tensor_copy(gain[:], gain_bank[:, 0:4])
+
+        own = [keep.tile([P, W], F32, name="own%d" % u) for u in range(4)]
+        far = [keep.tile([P, W], F32, name="far%d" % u, tag="root3" if u == 1 else "far%d" % u) for u in range(4)]
+        d = [keep.tile([P, S], F32, name="d%d" % u) for u in range(4)]
+        for u in range(4):
+            bank = bank_of("yb", "row", u)
+            product(bank[:], w1_q, u, xo)
+            nc.vector.tensor_scalar(m1[u][:, :S], bank[:], gain[:, u : u + 1], None, ALU.mult)
+        d_banks = []
+        for u in range(4):
+            d_banks.append(bank_of("db", "row", u))
+            product(d_banks[u][:], w2_q, u, xt)
+        for u in range(4):
+            fetch_vector(own[u][:], m1[u], n1_t[:], -0.5)
+
+        z_turned = keep.tile([P, 4, H], BF16, name="z_turned")
+        nums = []
+
+        def put(u):
+            nc.vector.tensor_tensor(m1[u][:].indirect(n1_t[:]), own[u][:], far[u][:], ALU.add)
+
+        def differ(u):
+            num = bank_of("num", "right" if u < 2 else "left", (u + 1) % 2)
+            turn_into(num, m1[u], True, False)
+            m1_far = h[u][:, S:]
+            if u < 3:
+                fetch_scalar(m1_far, m1[u], n3_t[:], -1.0)
+            else:
+                fetch_scalar(m1_far[:, cols(0)], m1[u], half_of(n3_t, 0), -1.0)
+                fetch_scalar(m1_far[:, cols(1)], m1[u], half_of(n3_t, 1), -1.0)
+            turn_into(num, m1_far, False, True)
+            nums.append(num)
+
+        def divide(u):
+            nc.vector.tensor_tensor(
+                z_turned[:].rearrange("p b (g u r) -> p u b g r", u=4, g=8)[:, u],
+                nums[u][:].rearrange("p (b g r) -> p b g r", b=4, g=8),
+                rec[u][:].rearrange("p (b g r) -> p b g r", b=4, g=8),
+                ALU.mult,
+            )
+
+        for u in range(2):
+            nc.vector.tensor_scalar(d[u][:], d_banks[u][:], gain[:, u : u + 1], None, ALU.mult)
+        nc.vector.tensor_copy(far[0][:], d[0][:].indirect(n2_t[:]))
+        fetch_scalar(far[1][:], d[1], n2_t[:], 1.0)
+        for u in range(2, 4):
+            nc.scalar.activation(d[u][:], d_banks[u][:], ACT.Copy, scale=gain[:, u : u + 1])
+        put(0)
+        put(1)
+        fetch_scalar(far[2][:], d[2], n2_t[:], 1.0)
+        differ(0)
+        fetch_scalar(far[3][:], d[3], n2_t[:], 1.0)
+        put(2)
+        differ(1)
+        divide(0)
+        put(3)
+        differ(2)
+        divide(1)
+        differ(3)
+        divide(2)
+        divide(3)
+
+        w4_g = keep.tile([P, N * PACK], BF16, name="w4_g", tag="m1_3", align_bytes=64)
+        nc.scalar.copy(
+            w4_g[:].rearrange("p (t m j) -> p m t j", t=4, j=PACK), w4_raw[:].rearrange("p j (m t) -> p m t j", t=4)
+        )
+        w4_q = quantise(w4_g[:], N, "w4")
+
+        z_q = []
+        z_words = z_turned[:].bitcast(F32)
+        for half in range(2):
+            back = bank_of("back", "right", 1 - half)[:].rearrange("p (b e j) -> p b e j", b=2, e=2)
+            for b in range(2):
+                for e in range(2):
+                    nc.tensor.transpose(back[:, b, e, :], z_words[:, 2 * half + b, e::2], ident[:])
+            z_g = keep.tile([P, HALF * PACK], BF16, name="z_g%d" % half, align_bytes=64)
+            copy = nc.scalar.copy if half == 0 else nc.vector.tensor_copy
+            copy(
+                z_g[:].bitcast(F32).rearrange("p (b j e) -> p b j e", b=2, e=2),
+                back.rearrange("p b e j -> p b j e"),
+            )
+            z_q.append(quantise(z_g[:], HALF, "z%d" % half))
+
+        out_rows = out.rearrange("(p t) j -> t p j", t=4)
+        banks = []
+        for t in range(4):
+            banks.append(bank_of("hb", "row", t))
+        for half in range(2):
+            for t in range(4):
+                product(banks[t][:, cols(half)], w4_q, t, z_q[half])
+        a = [keep.tile([P, S], F32, name="a%d" % t) for t in range(4)]
+        b = [keep.tile([P, S], F32, name="b%d" % t) for t in range(4)]
+        c = [keep.tile([P, S], F32, name="c%d" % t) for t in range(4)]
+        both = [keep.tile([P, S], F32, name="both%d" % t) for t in range(4)]
+
+        def leave(t):
+            (nc.vector.tensor_copy if t == 1 else nc.scalar.copy)(h[t][:, :S], banks[t][:])
+
+        def pieces(t):
+            if t < 3:
+                return [(slice(0, S), slice(0, S // 16))]
+            return [(cols(k), slice(k * HALF // 16, (k + 1) * HALF // 16)) for k in range(2)]
+
+        def rivals(t):
+            for cs, ls in pieces(t):
+                fetch_scalar(a[t][:, cs], h[t], n6_t[:, ls], 1.0)
+                fetch_scalar(b[t][:, cs], h[t], n7_t[:, ls], 1.0)
+
+        def fetch_near(t):
+            nc.vector.tensor_copy(c[t][:], h[t][:].indirect(n5_t[:]))
+
+        def add_own(t):
+            nc.vector.tensor_tensor(both[t][:], c[t][:], h[t][:, :S], ALU.add)
+
+        def finish(t):
+            top = work.tile([P, S], F32, name="top")
+            res = work.tile([P, S], F32, name="res")
+            for cs, ls in pieces(t):
+                nc.vector.tensor_tensor(top[:, cs], a[t][:, cs], b[t][:, cs], ALU.max)
+                nc.vector.tensor_tensor(res[:, cs], both[t][:, cs], top[:, cs], ALU.subtract)
+                nc.sync.dma_start(out_rows[t][:, cs], res[:, cs])
+
+        leave(0)
+        leave(1)
+        fetch_near(0)
+        add_own(0)
+        for t in range(4):
+            rivals(t)
+            if t + 2 < 4:
+                leave(t + 2)
+            if t + 1 < 4:
+                fetch_near(t + 1)
+            finish(t)
+            if t + 1 < 4:
+                add_own(t + 1)

@@ -62,8 +62,8 @@ def tile_picked_trioputbnormbtrim_none_p_kernel(
         offs_t = load_list(offs, "offs_t")
         w1_raw.append(load_weight_half(w1, 1, "w1_raw1"))
         n4_t = load_list(n4, "n4_t")
-        two_t = load_list(two, "two_t")
         w2_raw = load_weight(w2, "w2_raw")
+        two_t = load_list(two, "two_t")
         gain_rows = keep.tile([P, P], F32, name="gain_rows")
         nc.gpsimd.memset(gain_rows[:], 0.0)
         nc.sync.dma_start(
@@ -78,6 +78,9 @@ def tile_picked_trioputbnormbtrim_none_p_kernel(
         n7_t = load_list(n7, "n7_t")
         ident = keep.tile([P, P], F32, name="ident")
         make_identity(nc, ident[:])
+        warm = keep.tile([P, 2], F32, name="warm")
+        nc.gpsimd.memset(warm[:, 0:1], 1.0)
+        nc.scalar.activation(warm[:, 1:2], warm[:, 0:1], ACT.Abs_reciprocal_sqrt)
 
         def pick_words(lst, name):
             words = keep.tile([P, S], U32, name=name, align_bytes=64)
@@ -96,8 +99,11 @@ def tile_picked_trioputbnormbtrim_none_p_kernel(
             dst = grouped[:].rearrange("p (u g r j) -> p g u r j", u=4, g=8, j=PACK)[:, g0 : g0 + groups]
             copy(dst, raw.rearrange("p j (g u r) -> p g u r j", g=groups, u=4))
 
-        def quantise(grouped, width, name):
-            codes = keep.tile([P, width], U32, name=name + "_codes", align_bytes=64)
+        def round_gpsimd(dst, src):
+            nc.gpsimd.tensor_scalar(dst, src, 1.0, 0.0, ALU.mult, ALU.add)
+
+        def quantise(grouped, width, name, tag=None):
+            codes = keep.tile([P, width], U32, name=name + "_codes", tag=tag or name + "_codes", align_bytes=64)
             plane = keep.tile([P, width], U8, name=name + "_plane", align_bytes=64)
             nc.vector.quantize_mx(out=codes[:].bitcast(FP8X4), scales=plane[:], in_=grouped)
             return codes, plane
@@ -117,12 +123,12 @@ def tile_picked_trioputbnormbtrim_none_p_kernel(
         def bank_of(name, group, k):
             return psum.tile([P, S], F32, name=name, tag="%s%d" % (group, k))
 
-        def turn_into(bank, src, first, last):
-            for jb in range(4):
+        def turn_into(bank, src, first, last, jbs=(0, 1, 2, 3)):
+            for jb in jbs:
                 blk = slice(jb * P, (jb + 1) * P)
                 nc.tensor.matmul(
                     bank[:, blk], lhsT=src[:, blk], rhs=ident[:], is_transpose=True,
-                    start=(first and jb == 0), stop=(last and jb == 3),
+                    start=(first and jb == jbs[0]), stop=(last and jb == jbs[-1]),
                 )
 
         def fetch_scalar(dst, window, lst, factor):
@@ -144,7 +150,7 @@ def tile_picked_trioputbnormbtrim_none_p_kernel(
 
         m1 = [keep.tile([P, 2 * S], F32, name="m1_%d" % u, align_bytes=64) for u in range(4)]
         h = [keep.tile([P, 2 * S], F32, name="h%d" % t) for t in range(4)]
-        rec = [keep.tile([P, S], F32, name="rec%d" % u) for u in range(4)]
+        rec = [keep.tile([P, S], F32, name="rec%d" % u, align_bytes=64) for u in range(4)]
         dens = []
 
         def sizes(u):
@@ -163,7 +169,10 @@ def tile_picked_trioputbnormbtrim_none_p_kernel(
         def invert(u):
             root = keep.tile([P, S], F32, name="root%d" % u)
             nc.scalar.activation(root[:], dens[u][:], ACT.Abs_reciprocal_sqrt, bias=0.5)
-            nc.scalar.activation(rec[u][:], root[:], ACT.Square)
+            if u in []:
+                nc.gpsimd.tensor_tensor(rec[u][:], root[:], root[:], ALU.mult)
+            else:
+                nc.scalar.activation(rec[u][:], root[:], ACT.Square)
 
         for u in range(4):
             sizes(u)
@@ -172,9 +181,9 @@ def tile_picked_trioputbnormbtrim_none_p_kernel(
         invert(3)
 
         xt = [pick_words(two_t, "xt_words"), pick_scales(two_t, "xt_plane")]
-        w2_g = grouped_tile("w2_g")
-        round_by_runs(nc.vector.tensor_copy, w2_g, w2_raw[:], 0, 8)
-        w2_q = quantise(w2_g[:], H, "w2")
+        w2_g = keep.tile([P, H * PACK], BF16, name="w2_g", tag="w1_g", align_bytes=64)
+        for g in range(0, 8, 2):
+            round_by_runs(round_gpsimd, w2_g, w2_raw[:, :, 64 * g : 64 * g + 128], g, 2)
 
         gain_bank = bank_of("gb", "row", 3)
         nc.tensor.transpose(gain_bank[:, 0:P], gain_rows[:], ident[:])
@@ -182,12 +191,18 @@ def tile_picked_trioputbnormbtrim_none_p_kernel(
         nc.vector.tensor_copy(gain[:], gain_bank[:, 0:4])
 
         own = [keep.tile([P, W], F32, name="own%d" % u) for u in range(4)]
-        far = [keep.tile([P, W], F32, name="far%d" % u, tag="root3" if u == 1 else "far%d" % u) for u in range(4)]
-        d = [keep.tile([P, S], F32, name="d%d" % u) for u in range(4)]
+        far = [keep.tile([P, W], F32, name="far%d" % u, tag={}.get(u, "far%d" % u)) for u in range(4)]
+        d = [keep.tile([P, S], F32, name="d%d" % u, tag={1: "root2", 2: "root3"}.get(u, "d%d" % u)) for u in range(4)]
         for u in range(4):
             bank = bank_of("yb", "row", u)
             product(bank[:], w1_q, u, xo)
             nc.vector.tensor_scalar(m1[u][:, :S], bank[:], gain[:, u : u + 1], None, ALU.mult)
+        w2_q = quantise(w2_g[:], H, "w2")
+        w4_g = keep.tile([P, N * PACK], BF16, name="w4_g", tag="w1_g", align_bytes=64)
+        w4_dst = w4_g[:].rearrange("p (t m j) -> p m t j", t=4, j=PACK)
+        w4_src = w4_raw[:].rearrange("p j (m t) -> p m t j", t=4)
+        for k in range(0, P, 32):
+            round_gpsimd(w4_dst[:, k : k + 32], w4_src[:, k : k + 32])
         d_banks = []
         for u in range(4):
             d_banks.append(bank_of("db", "row", u))
@@ -201,82 +216,89 @@ def tile_picked_trioputbnormbtrim_none_p_kernel(
         def put(u):
             nc.vector.tensor_tensor(m1[u][:].indirect(n1_t[:]), own[u][:], far[u][:], ALU.add)
 
-        def differ(u):
-            num = bank_of("num", "right" if u < 2 else "left", (u + 1) % 2)
-            turn_into(num, m1[u], True, False)
+        def differ(u, jbs, bank, fetch=fetch_scalar):
+            cs = slice(jbs[0] * P, (jbs[-1] + 1) * P)
             m1_far = h[u][:, S:]
-            if u < 3:
-                fetch_scalar(m1_far, m1[u], n3_t[:], -1.0)
-            else:
-                fetch_scalar(m1_far[:, cols(0)], m1[u], half_of(n3_t, 0), -1.0)
-                fetch_scalar(m1_far[:, cols(1)], m1[u], half_of(n3_t, 1), -1.0)
-            turn_into(num, m1_far, False, True)
-            nums.append(num)
+            turn_into(bank, m1[u], True, False, jbs)
+            fetch(m1_far[:, cs], m1[u], n3_t[:, cs.start // 16 : cs.stop // 16], -1.0)
+            turn_into(bank, m1_far, False, True, jbs)
 
-        def divide(u):
+        def divide(u, jbs, bank):
+            cs = slice(jbs[0] * P, (jbs[-1] + 1) * P)
             nc.vector.tensor_tensor(
-                z_turned[:].rearrange("p b (g u r) -> p u b g r", u=4, g=8)[:, u],
-                nums[u][:].rearrange("p (b g r) -> p b g r", b=4, g=8),
-                rec[u][:].rearrange("p (b g r) -> p b g r", b=4, g=8),
+                z_turned[:].rearrange("p b (g u r) -> p u b g r", u=4, g=8)[:, u, jbs[0] : jbs[-1] + 1],
+                bank[:, cs].rearrange("p (b g r) -> p b g r", r=16, g=8),
+                rec[u][:, cs].rearrange("p (b g r) -> p b g r", r=16, g=8),
                 ALU.mult,
             )
 
-        for u in range(2):
-            nc.vector.tensor_scalar(d[u][:], d_banks[u][:], gain[:, u : u + 1], None, ALU.mult)
-        nc.vector.tensor_copy(far[0][:], d[0][:].indirect(n2_t[:]))
-        fetch_scalar(far[1][:], d[1], n2_t[:], 1.0)
-        for u in range(2, 4):
-            nc.scalar.activation(d[u][:], d_banks[u][:], ACT.Copy, scale=gain[:, u : u + 1])
+        def leave_d(u, on_vector):
+            if on_vector:
+                nc.vector.tensor_scalar(d[u][:], d_banks[u][:], gain[:, u : u + 1], None, ALU.mult)
+            else:
+                nc.scalar.activation(d[u][:], d_banks[u][:], ACT.Copy, scale=gain[:, u : u + 1])
+
+        def fetch_far(u, on_vector):
+            (fetch_vector if on_vector else fetch_scalar)(far[u][:], d[u], n2_t[:], 1.0)
+
+        whole, first, second = (0, 1, 2, 3), (0, 1), (2, 3)
+        leave_d(0, True)
+        fetch_far(0, True)
+        leave_d(1, False)
+        leave_d(2, False)
+        fetch_far(1, False)
+        leave_d(3, False)
+        fetch_far(2, False)
+        fetch_far(3, False)
         put(0)
         put(1)
-        fetch_scalar(far[2][:], d[2], n2_t[:], 1.0)
-        differ(0)
-        fetch_scalar(far[3][:], d[3], n2_t[:], 1.0)
+        num0 = bank_of("num0", "right", 1)
+        differ(0, whole, num0)
         put(2)
-        differ(1)
-        divide(0)
+        num1 = bank_of("num1", "right", 0)
+        differ(1, whole, num1)
+
         put(3)
-        differ(2)
-        divide(1)
-        differ(3)
-        divide(2)
-        divide(3)
+        num2 = bank_of("num2", "left", 1)
+        differ(2, whole, num2)
+        divide(0, whole, num0)
+        num3b = bank_of("num3b", "row", 0)
+        differ(3, second, num3b, fetch_scalar)
+        divide(1, whole, num1)
+        num3a = bank_of("num3a", "left", 0)
+        differ(3, first, num3a)
+        divide(2, whole, num2)
+        divide(3, second, num3b)
+        divide(3, first, num3a)
 
-        w4_g = keep.tile([P, N * PACK], BF16, name="w4_g", tag="m1_3", align_bytes=64)
-        nc.scalar.copy(
-            w4_g[:].rearrange("p (t m j) -> p m t j", t=4, j=PACK), w4_raw[:].rearrange("p j (m t) -> p m t j", t=4)
-        )
-        w4_q = quantise(w4_g[:], N, "w4")
+        w4_q = quantise(w4_g[:], N, "w4", "rec3")
 
-        z_q = []
+        z_q = {}
         z_words = z_turned[:].bitcast(F32)
-        for half in range(2):
-            back = bank_of("back", "right", 1 - half)[:].rearrange("p (b e j) -> p b e j", b=2, e=2)
+        for half in (1, 0):
+            back = bank_of("back", "right" if half == 1 else "left", 1 - half)[:].rearrange("p (b e j) -> p b e j", b=2, e=2)
             for b in range(2):
                 for e in range(2):
                     nc.tensor.transpose(back[:, b, e, :], z_words[:, 2 * half + b, e::2], ident[:])
             z_g = keep.tile([P, HALF * PACK], BF16, name="z_g%d" % half, align_bytes=64)
-            copy = nc.scalar.copy if half == 0 else nc.vector.tensor_copy
+            copy = nc.scalar.copy
             copy(
                 z_g[:].bitcast(F32).rearrange("p (b j e) -> p b j e", b=2, e=2),
                 back.rearrange("p b e j -> p b j e"),
             )
-            z_q.append(quantise(z_g[:], HALF, "z%d" % half))
+            z_q[half] = quantise(z_g[:], HALF, "z%d" % half)
 
         out_rows = out.rearrange("(p t) j -> t p j", t=4)
-        banks = []
-        for t in range(4):
-            banks.append(bank_of("hb", "row", t))
-        for half in range(2):
+        spare = [("right", 1), ("left", 0), ("right", 0), ("left", 1)]
+        for half in (1, 0):
             for t in range(4):
-                product(banks[t][:, cols(half)], w4_q, t, z_q[half])
+                bank = bank_of("hb", "row", t) if half == 1 else bank_of("hb", *spare[t])
+                product(bank[:, :HALF], w4_q, t, z_q[half])
+                (nc.vector.tensor_copy if t in (1, 2) else nc.scalar.copy)(h[t][:, cols(half)], bank[:, :HALF])
         a = [keep.tile([P, S], F32, name="a%d" % t) for t in range(4)]
         b = [keep.tile([P, S], F32, name="b%d" % t) for t in range(4)]
         c = [keep.tile([P, S], F32, name="c%d" % t) for t in range(4)]
         both = [keep.tile([P, S], F32, name="both%d" % t) for t in range(4)]
-
-        def leave(t):
-            (nc.vector.tensor_copy if t == 1 else nc.scalar.copy)(h[t][:, :S], banks[t][:])
 
         def pieces(t):
             if t < 3:
@@ -292,26 +314,19 @@ def tile_picked_trioputbnormbtrim_none_p_kernel(
             nc.vector.tensor_copy(c[t][:], h[t][:].indirect(n5_t[:]))
 
         def add_own(t):
-            nc.vector.tensor_tensor(both[t][:], c[t][:], h[t][:, :S], ALU.add)
+            (nc.gpsimd if t < 3 else nc.vector).tensor_tensor(both[t][:], c[t][:], h[t][:, :S], ALU.add)
 
         def finish(t):
-            top = work.tile([P, S], F32, name="top")
-            res = work.tile([P, S], F32, name="res")
+            top = keep.tile([P, S], F32, name="top%d" % t)
+            res = keep.tile([P, S], F32, name="res%d" % t)
             for cs, ls in pieces(t):
                 nc.vector.tensor_tensor(top[:, cs], a[t][:, cs], b[t][:, cs], ALU.max)
                 nc.vector.tensor_tensor(res[:, cs], both[t][:, cs], top[:, cs], ALU.subtract)
                 nc.sync.dma_start(out_rows[t][:, cs], res[:, cs])
 
-        leave(0)
-        leave(1)
-        fetch_near(0)
-        add_own(0)
+        for t in range(4):
+            fetch_near(t)
+            add_own(t)
         for t in range(4):
             rivals(t)
-            if t + 2 < 4:
-                leave(t + 2)
-            if t + 1 < 4:
-                fetch_near(t + 1)
             finish(t)
-            if t + 1 < 4:
-                add_own(t + 1)

from contextlib import ExitStack

import concourse.mybir as mybir
from concourse.masks import make_identity

F32 = mybir.dt.float32
BF16 = mybir.dt.bfloat16
I32 = mybir.dt.int32
U32 = mybir.dt.uint32
U16 = mybir.dt.uint16
U8 = mybir.dt.uint8
FP8X4 = mybir.dt.float8_e4m3fn_x4
ALU = mybir.AluOpType
ACT = mybir.ActivationFunctionType

P = 128
PACK = 4
K, T, S, H, N, W = 512, 2048, 512, 512, 512, 256
HALF = S // 2
FLOPS = 2 * (3 * K * H * S + H * N * S)


def tile_picked_trioputbnormbtrim_none_p_kernel(
    tc, x_words, x_scales, w1, w2, w3, gn, w4, offs, two, three, n1, n2, n3, n4, n5, n6, n7, out
):
    nc = tc.nc
    with ExitStack() as ctx:
        keep = ctx.enter_context(tc.tile_pool(name="keep", bufs=1))
        work = ctx.enter_context(tc.tile_pool(name="work", bufs=2))
        psum = ctx.enter_context(tc.psum_pool(name="psum", bufs=1))

        def load_list(src, name):
            tile = keep.tile(list(src.shape), U16, name=name)
            nc.sync.dma_start(tile[:], src)
            return tile

        def load_weight_half(w, half, name):
            raw = keep.tile([P, PACK, HALF], F32, name=name)
            nc.sync.dma_start(raw[:], w.rearrange("(p j) c -> p j c", j=PACK)[:, :, half * HALF : (half + 1) * HALF])
            return raw

        def load_weight(w, name):
            raw = keep.tile([P, PACK, H], F32, name=name)
            nc.sync.dma_start(raw[:], w.rearrange("(p j) c -> p j c", j=PACK))
            return raw

        def half_of(lst, half):
            return lst[:, half * (HALF // 16) : (half + 1) * (HALF // 16)]

        def cols(half):
            return slice(half * HALF, (half + 1) * HALF)

        x_plane = keep.tile([P, T], U8, name="x_plane", align_bytes=64)
        nc.vector.memset(x_plane[:].bitcast(I32), 0)
        three_t = load_list(three, "three_t")
        x_codes = keep.tile([P, T], U32, name="x_codes", align_bytes=64)
        nc.sync.dma_start(x_codes[:].bitcast(I32), x_words[0].rearrange("p n t -> p (n t)").bitcast(I32))
        for q in range(4):
            nc.scalar.dma_start(x_plane[32 * q : 32 * q + 4, :].bitcast(I32), x_scales[0, 4 * q : 4 * q + 4, :].bitcast(I32))
        w3_raw = [load_weight_half(w3, h, "w3_raw%d" % h) for h in range(2)]
        w1_raw = [load_weight_half(w1, 0, "w1_raw0")]
        offs_t = load_list(offs, "offs_t")
        w1_raw.append(load_weight_half(w1, 1, "w1_raw1"))
        n4_t = load_list(n4, "n4_t")
        w2_raw = load_weight(w2, "w2_raw")
        two_t = load_list(two, "two_t")
        gain_rows = keep.tile([P, P], F32, name="gain_rows")
        nc.gpsimd.memset(gain_rows[:], 0.0)
        nc.sync.dma_start(
            gain_rows[0:4, :].rearrange("u (g r) -> u g r", g=8), gn.rearrange("(g u r) o -> u g (r o)", g=8, u=4)
        )
        n1_t = load_list(n1, "n1_t")
        n2_t = load_list(n2, "n2_t")
        w4_raw = load_weight(w4, "w4_raw")
        n3_t = load_list(n3, "n3_t")
        n5_t = load_list(n5, "n5_t")
        n6_t = load_list(n6, "n6_t")
        n7_t = load_list(n7, "n7_t")
        ident = keep.tile([P, P], F32, name="ident")
        make_identity(nc, ident[:])
        warm = keep.tile([P, 2], F32, name="warm")
        nc.gpsimd.memset(warm[:, 0:1], 1.0)
        nc.scalar.activation(warm[:, 1:2], warm[:, 0:1], ACT.Abs_reciprocal_sqrt)

        def pick_words(lst, name):
            words = keep.tile([P, S], U32, name=name, align_bytes=64)
            nc.vector.tensor_copy(words[:], x_codes[:].indirect(lst[:]))
            return words

        def pick_scales(lst, name):
            plane = keep.tile([P, S], U8, name=name, align_bytes=64)
            nc.vector.tensor_copy(plane[:], x_plane[:].indirect(lst[:]))
            return plane

        def grouped_tile(name):
            return keep.tile([P, H * PACK], BF16, name=name, align_bytes=64)

        def round_by_runs(copy, grouped, raw, g0, groups):
            dst = grouped[:].rearrange("p (u g r j) -> p g u r j", u=4, g=8, j=PACK)[:, g0 : g0 + groups]
            copy(dst, raw.rearrange("p j (g u r) -> p g u r j", g=groups, u=4))

        def round_gpsimd(dst, src):
            nc.gpsimd.tensor_scalar(dst, src, 1.0, 0.0, ALU.mult, ALU.add)

        def quantise(grouped, width, name, tag=None):
            codes = keep.tile([P, width], U32, name=name + "_codes", tag=tag or name + "_codes", align_bytes=64)
            plane = keep.tile([P, width], U8, name=name + "_plane", align_bytes=64)
            nc.vector.quantize_mx(out=codes[:].bitcast(FP8X4), scales=plane[:], in_=grouped)
            return codes, plane

        def product(acc, weights, u, moving):
            m = slice(u * P, (u + 1) * P)
            nc.tensor.matmul_mx(
                out=acc,
                lhsT=weights[0][:, m].bitcast(FP8X4),
                lhsT_scale=weights[1][:, m],
                rhs=moving[0][:].bitcast(FP8X4),
                rhs_scale=moving[1][:],
                start=True,
                stop=True,
            )

        def bank_of(name, group, k):
            return psum.tile([P, S], F32, name=name, tag="%s%d" % (group, k))

        def turn_into(bank, src, first, last, jbs=(0, 1, 2, 3)):
            for jb in jbs:
                blk = slice(jb * P, (jb + 1) * P)
                nc.tensor.matmul(
                    bank[:, blk], lhsT=src[:, blk], rhs=ident[:], is_transpose=True,
                    start=(first and jb == jbs[0]), stop=(last and jb == jbs[-1]),
                )

        def fetch_scalar(dst, window, lst, factor):
            nc.scalar.activation(dst, window[:].indirect(lst), ACT.Copy, scale=factor)

        def fetch_vector(dst, window, lst, factor):
            nc.vector.tensor_scalar(dst, window[:].indirect(lst), factor, 0.0, ALU.mult, ALU.add)

        x3 = [pick_words(three_t, "x3_words"), pick_scales(three_t, "x3_plane")]
        w3_g = grouped_tile("w3_g")
        round_by_runs(nc.scalar.copy, w3_g, w3_raw[0][:], 0, 4)
        round_by_runs(nc.vector.tensor_copy, w3_g, w3_raw[1][:], 4, 4)
        w3_q = quantise(w3_g[:], H, "w3")
        w1_g = grouped_tile("w1_g")
        round_by_runs(nc.scalar.copy, w1_g, w1_raw[0][:], 0, 4)
        xo = [pick_words(offs_t, "xo_words"), pick_scales(offs_t, "xo_plane")]
        round_by_runs(nc.vector.tensor_copy, w1_g, w1_raw[1][:], 4, 4)
        w1_q = quantise(w1_g[:], H, "w1")

        m1 = [keep.tile([P, 2 * S], F32, name="m1_%d" % u, align_bytes=64) for u in range(4)]
        h = [keep.tile([P, 2 * S], F32, name="h%d" % t) for t in range(4)]
        rec = [keep.tile([P, S], F32, name="rec%d" % u, align_bytes=64) for u in range(4)]
        dens = []

        def sizes(u):
            bank = bank_of("bb", "left", u % 2)
            product(bank[:], w3_q, u, x3)
            size = work.tile([P, S], F32, name="size")
            nc.scalar.activation(size[:], bank[:], ACT.Abs)
            size_far = m1[u][:, S:]
            for half in range(2):
                fetch_scalar(size_far[:, cols(half)], size, half_of(n4_t, half), 1.0)
            den = bank_of("den", "right", u % 2)
            turn_into(den, size, True, False)
            turn_into(den, size_far, False, True)
            dens.append(den)

        def invert(u):
            root = keep.tile([P, S], F32, name="root%d" % u)
            nc.scalar.activation(root[:], dens[u][:], ACT.Abs_reciprocal_sqrt, bias=0.5)
            if u in []:
                nc.gpsimd.tensor_tensor(rec[u][:], root[:], root[:], ALU.mult)
            else:
                nc.scalar.activation(rec[u][:], root[:], ACT.Square)

        for u in range(4):
            sizes(u)
            if u > 0:
                invert(u - 1)
        invert(3)

        xt = [pick_words(two_t, "xt_words"), pick_scales(two_t, "xt_plane")]
        w2_g = keep.tile([P, H * PACK], BF16, name="w2_g", tag="w1_g", align_bytes=64)
        for g in range(0, 8, 2):
            round_by_runs(round_gpsimd, w2_g, w2_raw[:, :, 64 * g : 64 * g + 128], g, 2)

        gain_bank = bank_of("gb", "row", 3)
        nc.tensor.transpose(gain_bank[:, 0:P], gain_rows[:], ident[:])
        gain = keep.tile([P, 4], F32, name="gain")
        nc.vector.tensor_copy(gain[:], gain_bank[:, 0:4])

        own = [keep.tile([P, W], F32, name="own%d" % u) for u in range(4)]
        far = [keep.tile([P, W], F32, name="far%d" % u, tag={}.get(u, "far%d" % u)) for u in range(4)]
        d = [keep.tile([P, S], F32, name="d%d" % u, tag={1: "root2", 2: "root3"}.get(u, "d%d" % u)) for u in range(4)]
        for u in range(4):
            bank = bank_of("yb", "row", u)
            product(bank[:], w1_q, u, xo)
            nc.vector.tensor_scalar(m1[u][:, :S], bank[:], gain[:, u : u + 1], None, ALU.mult)
        w2_q = quantise(w2_g[:], H, "w2")
        w4_g = keep.tile([P, N * PACK], BF16, name="w4_g", tag="w1_g", align_bytes=64)
        w4_dst = w4_g[:].rearrange("p (t m j) -> p m t j", t=4, j=PACK)
        w4_src = w4_raw[:].rearrange("p j (m t) -> p m t j", t=4)
        for k in range(0, P, 32):
            round_gpsimd(w4_dst[:, k : k + 32], w4_src[:, k : k + 32])
        d_banks = []
        for u in range(4):
            d_banks.append(bank_of("db", "row", u))
            product(d_banks[u][:], w2_q, u, xt)
        for u in range(4):
            fetch_vector(own[u][:], m1[u], n1_t[:], -0.5)

        z_turned = keep.tile([P, 4, H], BF16, name="z_turned")
        nums = []

        def put(u):
            nc.vector.tensor_tensor(m1[u][:].indirect(n1_t[:]), own[u][:], far[u][:], ALU.add)

        def differ(u, jbs, bank, fetch=fetch_scalar):
            cs = slice(jbs[0] * P, (jbs[-1] + 1) * P)
            m1_far = h[u][:, S:]
            turn_into(bank, m1[u], True, False, jbs)
            fetch(m1_far[:, cs], m1[u], n3_t[:, cs.start // 16 : cs.stop // 16], -1.0)
            turn_into(bank, m1_far, False, True, jbs)

        def divide(u, jbs, bank):
            cs = slice(jbs[0] * P, (jbs[-1] + 1) * P)
            nc.vector.tensor_tensor(
                z_turned[:].rearrange("p b (g u r) -> p u b g r", u=4, g=8)[:, u, jbs[0] : jbs[-1] + 1],
                bank[:, cs].rearrange("p (b g r) -> p b g r", r=16, g=8),
                rec[u][:, cs].rearrange("p (b g r) -> p b g r", r=16, g=8),
                ALU.mult,
            )

        def leave_d(u, on_vector):
            if on_vector:
                nc.vector.tensor_scalar(d[u][:], d_banks[u][:], gain[:, u : u + 1], None, ALU.mult)
            else:
                nc.scalar.activation(d[u][:], d_banks[u][:], ACT.Copy, scale=gain[:, u : u + 1])

        def fetch_far(u, on_vector):
            (fetch_vector if on_vector else fetch_scalar)(far[u][:], d[u], n2_t[:], 1.0)

        whole, first, second = (0, 1, 2, 3), (0, 1), (2, 3)
        leave_d(0, True)
        fetch_far(0, True)
        leave_d(1, False)
        leave_d(2, False)
        fetch_far(1, False)
        leave_d(3, False)
        fetch_far(2, False)
        fetch_far(3, False)
        put(0)
        put(1)
        num0 = bank_of("num0", "right", 1)
        differ(0, whole, num0)
        put(2)
        num1 = bank_of("num1", "right", 0)
        differ(1, whole, num1)

        put(3)
        num2 = bank_of("num2", "left", 1)
        differ(2, whole, num2)
        divide(0, whole, num0)
        num3b = bank_of("num3b", "row", 0)
        differ(3, second, num3b, fetch_scalar)
        divide(1, whole, num1)
        num3a = bank_of("num3a", "left", 0)
        differ(3, first, num3a)
        divide(2, whole, num2)
        divide(3, second, num3b)
        divide(3, first, num3a)

        w4_q = quantise(w4_g[:], N, "w4", "rec3")

        z_q = {}
        z_words = z_turned[:].bitcast(F32)
        for half in (1, 0):
            back = bank_of("back", "right" if half == 1 else "left", 1 - half)[:].rearrange("p (b e j) -> p b e j", b=2, e=2)
            for b in range(2):
                for e in range(2):
                    nc.tensor.transpose(back[:, b, e, :], z_words[:, 2 * half + b, e::2], ident[:])
            z_g = keep.tile([P, HALF * PACK], BF16, name="z_g%d" % half, align_bytes=64)
            copy = nc.scalar.copy
            copy(
                z_g[:].bitcast(F32).rearrange("p (b j e) -> p b j e", b=2, e=2),
                back.rearrange("p b e j -> p b j e"),
            )
            z_q[half] = quantise(z_g[:], HALF, "z%d" % half)

        out_rows = out.rearrange("(p t) j -> t p j", t=4)
        spare = [("right", 1), ("left", 0), ("right", 0), ("left", 1)]
        for half in (1, 0):
            for t in range(4):
                bank = bank_of("hb", "row", t) if half == 1 else bank_of("hb", *spare[t])
                product(bank[:, :HALF], w4_q, t, z_q[half])
                (nc.vector.tensor_copy if t in (1, 2) else nc.scalar.copy)(h[t][:, cols(half)], bank[:, :HALF])
        a = [keep.tile([P, S], F32, name="a%d" % t) for t in range(4)]
        b = [keep.tile([P, S], F32, name="b%d" % t) for t in range(4)]
        c = [keep.tile([P, S], F32, name="c%d" % t) for t in range(4)]
        both = [keep.tile([P, S], F32, name="both%d" % t) for t in range(4)]

        def pieces(t):
            if t < 3:
                return [(slice(0, S), slice(0, S // 16))]
            return [(cols(k), slice(k * HALF // 16, (k + 1) * HALF // 16)) for k in range(2)]

        def rivals(t):
            for cs, ls in pieces(t):
                fetch_scalar(a[t][:, cs], h[t], n6_t[:, ls], 1.0)
                fetch_scalar(b[t][:, cs], h[t], n7_t[:, ls], 1.0)

        def fetch_near(t):
            nc.vector.tensor_copy(c[t][:], h[t][:].indirect(n5_t[:]))

        def add_own(t):
            (nc.gpsimd if t < 3 else nc.vector).tensor_tensor(both[t][:], c[t][:], h[t][:, :S], ALU.add)

        def finish(t):
            top = keep.tile([P, S], F32, name="top%d" % t)
            res = keep.tile([P, S], F32, name="res%d" % t)
            for cs, ls in pieces(t):
                nc.vector.tensor_tensor(top[:, cs], a[t][:, cs], b[t][:, cs], ALU.max)
                nc.vector.tensor_tensor(res[:, cs], both[t][:, cs], top[:, cs], ALU.subtract)
                nc.sync.dma_start(out_rows[t][:, cs], res[:, cs])

        for t in range(4):
            fetch_near(t)
            add_own(t)
        for t in range(4):
            rivals(t)
            finish(t)
